import numpy as np
import ml_dtypes


def mxq(x, axis, fmt="e4m3"):
    dtype, down = {"e4m3": (ml_dtypes.float8_e4m3fn, 7), "e5m2": (ml_dtypes.float8_e5m2, 14)}[fmt]
    v = np.moveaxis(np.asarray(x, np.float32).astype(ml_dtypes.bfloat16).astype(np.float64), axis, -1)
    blocks = v.reshape(v.shape[:-1] + (-1, 32))
    amax = np.abs(blocks).max(-1, keepdims=True)
    byte = np.maximum(np.where(amax > 0, np.frexp(amax)[1] - 1 + 127, 0) - down, 1)
    scale = np.exp2(byte - 127.0)
    codes = (blocks / scale).astype(np.float32).astype(dtype).astype(np.float64)
    return np.moveaxis((codes * scale).reshape(v.shape), -1, axis)


WIDE = False


def mx_kscale(k):
    if not WIDE:
        return np.ones(k)
    levels = np.array([10, -10, 5, -5, 0])
    if k % 512:
        return np.exp2(np.random.permutation(np.resize(levels, k // 32))).repeat(32)
    a = np.empty((k // 512, 16))
    for p in range(k // 512):
        a[p, :8] = np.random.permutation(np.resize(levels, 8))
        for g in range(8):
            far = levels[np.abs(levels - a[p, g]) >= 10]
            a[p, g + 8] = far[np.random.randint(len(far))]
    return np.exp2(a.ravel()).repeat(32)


def f64(x):
    return np.asarray(x).astype(np.float64)


def striped(idx):
    return np.tile(np.asarray(idx).reshape(-1, 16).T, (8, 1)).astype(np.uint16)


def unstriped(offs):
    return offs[:16].T.reshape(-1).astype(np.int64)


E2M1 = np.array([0.0, 0.5, 1.0, 1.5, 2.0, 3.0, 4.0, 6.0, -0.0, -0.5, -1.0, -1.5, -2.0, -3.0, -4.0, -6.0])


def pack_weight(w, fmt):
    k, n = w.shape
    w = f64(np.asarray(w, np.float32).astype(ml_dtypes.bfloat16)).reshape(k // 32, 32, n)
    amax = np.abs(w).max(1)
    if fmt == "e4m3":
        byte = np.frexp(amax)[1] - 1 + 127 - 7
    else:
        mant, ex = np.frexp(amax / 6.0)
        byte = np.where(mant > 0.5, ex, ex - 1) + 127
    byte = np.clip(np.where(amax > 0, byte, 1), 1, 254)
    scaled = (w * np.exp2(127.0 - byte)[:, None, :]).reshape(k, n).astype(np.float32)
    by_word = np.ascontiguousarray(scaled.reshape(k // 512, 128, 4, n).transpose(0, 1, 3, 2))
    if fmt == "e4m3":
        words = by_word.astype(ml_dtypes.float8_e4m3fn).view(np.uint8)
    else:
        c = by_word.astype(ml_dtypes.float4_e2m1fn).view(np.uint8) & 0xF
        words = (c[..., 0::2] | (c[..., 1::2] << 4)).reshape(k // 512, 128, 2 * n)
    return np.ascontiguousarray(words), np.ascontiguousarray(byte.astype(np.uint8).reshape(k // 512, 16, n))


def unpack_weight(words, scales, fmt):
    g, _, n = scales.shape
    words = np.ascontiguousarray(words).reshape(g, 128, n, -1)
    if fmt == "e4m3":
        vals = words.view(ml_dtypes.float8_e4m3fn).astype(np.float64)
    else:
        nib = np.empty((g, 128, n, 4), np.uint8)
        nib[..., 0::2] = words & 0xF
        nib[..., 1::2] = words >> 4
        vals = E2M1[nib]
    vals = vals * np.repeat(np.exp2(scales.astype(np.float64) - 127.0), 8, axis=1)[..., None]
    return vals.transpose(0, 1, 3, 2).reshape(g * 512, n)


D, E, T, I, Q = 512, 512, 2048, 512, 128


def setup_inputs():
    n = np.random.standard_normal
    idx = np.random.permutation(T)[:I]
    fd = mx_kscale(D)
    fe = mx_kscale(E)
    keysp = pack_weight(n((D, T)) / fd[:, None], "e2m1")
    valsp = pack_weight(n((E, T)) / fe[:, None], "e2m1")
    return {
        "query": (n((D, Q)) * 0.9 / np.sqrt(D) * fd[:, None]).astype(np.float32),
        "query2": (n((D, Q)) * 0.6 / np.sqrt(D) * fd[:, None]).astype(np.float32),
        "keys_words": keysp[0],
        "keys_scales": keysp[1],
        "gout": (n((E, Q)) * 1 / np.sqrt(E) * fe[:, None]).astype(np.float32),
        "vals_words": valsp[0],
        "vals_scales": valsp[1],
        "size": (np.random.uniform(0.5, 2.0, (1, I))).astype(np.float32),
        "dquery": (n((D, Q)) * 1.0 / np.sqrt(D) * fd[:, None]).astype(np.float32),
        "base": (0.5 * n((Q, T))).astype(np.float32),
        "offs": striped(idx),
    }


def reference(query, query2, keys_words, keys_scales, gout, vals_words, vals_scales, size, dquery, base, offs):
    idx = unstriped(offs)
    keysu = unpack_weight(keys_words, keys_scales, "e2m1")
    valsu = unpack_weight(vals_words, vals_scales, "e2m1")
    queryq = mxq(f64(query), 0, "e4m3")
    keysidxg = keysu[:, idx]
    a = queryq.T @ keysidxg
    dqueryq = mxq(f64(dquery), 0, "e4m3")
    ta = dqueryq.T @ keysidxg
    query2q = mxq(f64(query2), 0, "e4m3")
    b = query2q.T @ keysidxg
    pa = np.exp(a - np.max(a, axis=1, keepdims=True))
    wa = pa / np.sum(pa, axis=1, keepdims=True)
    pb = np.exp(b - np.max(b, axis=1, keepdims=True))
    wb = pb / np.sum(pb, axis=1, keepdims=True)
    goutq = mxq(f64(gout), 0, "e4m3")
    valsidxg = valsu[:, idx]
    c0 = goutq.T @ valsidxg
    dwa = c0 * f64(size) / (wa + wb) * wb - c0 * f64(size) * wa * wb / np.square(wa + wb)
    dpa = dwa / np.sum(pa, axis=1, keepdims=True) + np.sum(dwa * pa / np.square(np.sum(pa, axis=1, keepdims=True)) * (-1.0), axis=1, keepdims=True)
    tpa = ta * pa
    twa = (tpa - np.sum(tpa, axis=1, keepdims=True) * pa / np.sum(pa, axis=1, keepdims=True)) / np.sum(pa, axis=1, keepdims=True)
    tdwa = twa * c0 * f64(size) / np.square(wa + wb) * (-1.0) * wb - (twa * wb * c0 * f64(size) - twa * (wa + wb) * 2.0 * c0 * f64(size) * wa * wb / np.square(wa + wb)) / np.square(wa + wb)
    tdpa = (tdwa - np.sum(tpa, axis=1, keepdims=True) * dwa / np.sum(pa, axis=1, keepdims=True)) / np.sum(pa, axis=1, keepdims=True) + np.sum((tdwa * pa + tpa * dwa - np.sum(tpa, axis=1, keepdims=True) * np.sum(pa, axis=1, keepdims=True) * 2.0 * dwa * pa / np.square(np.sum(pa, axis=1, keepdims=True))) / np.square(np.sum(pa, axis=1, keepdims=True)) * (-1.0), axis=1, keepdims=True)
    tda = tdpa * pa + tpa * dpa
    gs = tda * 512.0
    gf = np.zeros((Q, T))
    gf[:, idx] = gs
    y = f64(base) + gf
    return y

@@ -1,0 +1,214 @@
+import math
+from contextlib import ExitStack
+
+import concourse.mybir as mybir
+from concourse.masks import make_identity
+
+D, T, I, Q = 512, 2048, 512, 128
+P = 128
+PACK = 4
+FLOPS = 4 * 2 * D * Q * I
+
+F32 = mybir.dt.float32
+BF16 = mybir.dt.bfloat16
+I32 = mybir.dt.int32
+U32 = mybir.dt.uint32
+U16 = mybir.dt.uint16
+U8 = mybir.dt.uint8
+FP8X4 = mybir.dt.float8_e4m3fn_x4
+FP4X4 = mybir.dt.float4_e2m1fn_x4
+ALU = mybir.AluOpType
+ACT = mybir.ActivationFunctionType
+
+TERMS = 36
+STEPS = TERMS + 4
+EXPONENT_BITS = 0x7F800000
+SIGN_AND_EXPONENT_BITS = -0x00800000
+OUT_CHUNK = 512
+
+
+def tile_attend_hvagreement_s_kernel(tc, query, query2, keys_words, keys_scales, gout, vals_words, vals_scales,
+                                      size, dquery, base, offs, out):
+    nc = tc.nc
+    with ExitStack() as ctx:
+        sb = ctx.enter_context(tc.tile_pool(name="sb", bufs=1))
+        ps = ctx.enter_context(tc.psum_pool(name="ps", bufs=1))
+
+        def tile(name, shape, dtype):
+            return sb.tile(shape, dtype, name=name, align_bytes=64)
+
+        def column(name):
+            return sb.tile([P, 1], F32, name=name)
+
+        offsets = sb.tile([P, I // 16], U16, name="offsets")
+        key_words = tile("key_words", [P, T], U16)
+        key_scales = tile("key_scales", [P, T], U8)
+        val_words = tile("val_words", [P, T], U16)
+        val_scales = tile("val_scales", [P, T], U8)
+        placed = tile("placed", [P, T], F32)
+        base_sb = tile("base_sb", [P, T], F32)
+        size_cols = tile("size_cols", [P, I // P], F32)
+
+        nc.vector.memset(key_scales[:].bitcast(I32), 0)
+        nc.vector.memset(val_scales[:].bitcast(I32), 0)
+
+        def load_words(dst, src):
+            nc.sync.dma_start(out=dst[:].bitcast(I32), in_=src[0].bitcast(I32))
+
+        def load_scales(dst, src):
+            for quad in range(4):
+                nc.sync.dma_start(out=dst[32 * quad:32 * quad + 4, :].bitcast(I32),
+                                  in_=src[0, 4 * quad:4 * quad + 4, :].bitcast(I32))
+
+        def load_rows(name, src):
+            raw = tile(name + "_raw", [P, PACK, Q], F32)
+            nc.sync.dma_start(out=raw[:], in_=src.rearrange("(p j) q -> p j q", j=PACK))
+            return raw
+
+        nc.sync.dma_start(offsets[:], offs)
+        load_words(key_words, keys_words)
+        load_scales(key_scales, keys_scales)
+        query_raw = load_rows("query", query)
+        query2_raw = load_rows("query2", query2)
+        dquery_raw = load_rows("dquery", dquery)
+        gout_raw = load_rows("gout", gout)
+        load_words(val_words, vals_words)
+        load_scales(val_scales, vals_scales)
+        with nc.allow_non_contiguous_dma(reason="one weight a partition"):
+            nc.sync.dma_start(out=size_cols[:], in_=size.rearrange("o (j s) -> s (o j)", s=P))
+        nc.sync.dma_start(out=base_sb[:], in_=base)
+
+        orders = tile("orders", [P, TERMS], F32)
+        nc.gpsimd.iota(orders[:], pattern=[[-1, TERMS]], base=TERMS, channel_multiplier=0,
+                       allow_small_or_imprecise_dtypes=True)
+        identity = tile("identity", [P, P], F32)
+        make_identity(nc, identity[:])
+        thirds = tile("thirds", [P, TERMS], F32)
+        nc.scalar.activation(thirds[:], orders[:], ACT.Exp, scale=-math.log(3.0))
+        factors = tile("factors", [P, STEPS], F32)
+        addends = tile("addends", [P, STEPS], F32)
+        inverse_orders = tile("inverse_orders", [P, TERMS], F32)
+        nc.vector.memset(placed[:], 0.0)
+        nc.vector.memset(factors[:, TERMS + 1:TERMS + 3], -1.0)
+        nc.vector.memset(factors[:, TERMS + 3:], 0.5)
+        nc.vector.memset(addends[:, TERMS + 3:], 0.0)
+        nc.vector.reciprocal(inverse_orders[:], orders[:])
+        nc.vector.tensor_tensor(addends[:, :TERMS], thirds[:], inverse_orders[:], ALU.mult)
+        half = factors[:, TERMS + 3:]
+        neg_max_a = addends[:, TERMS + 1:TERMS + 2]
+        neg_max_b = addends[:, TERMS + 2:TERMS + 3]
+
+        def interleave(name, raw):
+            grouped = tile(name + "_grouped", [P, Q, PACK], BF16)
+            nc.scalar.copy(grouped[:].rearrange("p (c i) j -> p c j i", i=4),
+                           raw[:].rearrange("p j (c i) -> p c j i", i=4))
+            return grouped
+
+        def quantize(name, grouped):
+            codes = tile(name + "_codes", [P, Q], U32)
+            scales = tile(name + "_scales", [P, Q], U8)
+            nc.vector.quantize_mx(out=codes[:].bitcast(FP8X4), scales=scales[:],
+                                  in_=grouped[:].rearrange("p q j -> p (q j)"))
+            return codes, scales
+
+        def gather(name, window, dtype):
+            picked = tile(name, [P, I], dtype)
+            nc.vector.tensor_copy(picked[:], window[:].indirect(offsets[:]))
+            return picked
+
+        def score(name, rows):
+            bank = ps.tile([P, I], F32, name=name)
+            nc.tensor.matmul_mx(out=bank[:], lhsT=rows[0][:].bitcast(FP8X4), lhsT_scale=rows[1][:],
+                                rhs=kw[:].bitcast(FP4X4), rhs_scale=ks[:], start=True, stop=True)
+            return bank
+
+        query_g = interleave("query", query_raw)
+        query2_g = interleave("query2", query2_raw)
+        dquery_g = interleave("dquery", dquery_raw)
+        gout_g = interleave("gout", gout_raw)
+
+        kw = gather("kw", key_words, U16)
+        ks = gather("ks", key_scales, U8)
+        a = score("a", quantize("query", query_g))
+        b = score("b", quantize("query2", query2_g))
+        ta = score("ta", quantize("dquery", dquery_g))
+        gout_codes, gout_scales = quantize("gout", gout_g)
+
+        neg_a = tile("neg_a", [P, I], F32)
+        neg_b = tile("neg_b", [P, I], F32)
+        nc.vector.tensor_scalar(neg_a[:], a[:], -1.0, None, op0=ALU.mult, op1=ALU.min, accum_out=neg_max_a)
+        nc.vector.tensor_scalar(neg_b[:], b[:], -1.0, None, op0=ALU.mult, op1=ALU.min, accum_out=neg_max_b)
+        pa = tile("pa", [P, I], F32)
+        pb = tile("pb", [P, I], F32)
+        sum_a = column("sum_a")
+        sum_b = column("sum_b")
+        nc.scalar.activation(pa[:], neg_a[:], ACT.Exp, bias=neg_max_a, scale=-1.0, accum_out=sum_a[:])
+        nc.scalar.activation(pb[:], neg_b[:], ACT.Exp, bias=neg_max_b, scale=-1.0, accum_out=sum_b[:])
+        gap = tile("gap", [P, I], F32)
+        nc.vector.tensor_tensor(gap[:], b[:], neg_a[:], ALU.add)
+        inv_a = column("inv_a")
+        nc.vector.reciprocal(inv_a[:], sum_a[:])
+        wa = tile("wa", [P, I], F32)
+        nc.scalar.activation(wa[:], pa[:], ACT.Copy, scale=inv_a[:])
+
+        ratio = column("ratio")
+        power = sb.tile([P, 1], I32, name="power")
+        nc.vector.tensor_tensor(ratio[:], sum_b[:], inv_a[:], ALU.mult)
+        nc.vector.tensor_scalar(power[:], ratio[:].bitcast(I32), EXPONENT_BITS, SIGN_AND_EXPONENT_BITS,
+                                op0=ALU.bitwise_and, op1=ALU.bitwise_xor)
+        nc.vector.tensor_scalar(factors[:, :TERMS + 1], ratio[:].to_broadcast([P, TERMS + 1]), power[:].bitcast(F32), 3.0,
+                                op0=ALU.mult, op1=ALU.add)
+        nc.vector.tensor_scalar(addends[:, TERMS:TERMS + 1], power[:], (129.0 - math.log2(3.0)) * 2.0 ** 23,
+                                math.log(2.0) / 2.0 ** 23, op0=ALU.add, op1=ALU.mult)
+        horner = tile("horner", [P, STEPS], F32)
+        nc.vector.tensor_tensor_scan(horner[:], factors[:], addends[:], 0.0, op0=ALU.mult, op1=ALU.add)
+        tanh = tile("tanh", [P, I], F32)
+        share_sq = tile("share_sq", [P, I], F32)
+        nc.scalar.activation(tanh[:], gap[:], ACT.Tanh, bias=horner[:, STEPS - 1:], scale=0.5)
+        nc.scalar.activation(share_sq[:], tanh[:], ACT.Square, bias=half, scale=0.5)
+
+        vw = gather("vw", val_words, U16)
+        vs = gather("vs", val_scales, U8)
+        c0_turned = ps.tile([P, I // P, Q], F32, name="c0_turned")
+        for j in range(I // P):
+            slots = slice(j * P, (j + 1) * P)
+            nc.tensor.matmul_mx(out=c0_turned[:, j, :], lhsT=vw[:, slots].bitcast(FP4X4), lhsT_scale=vs[:, slots],
+                                rhs=gout_codes[:].bitcast(FP8X4), rhs_scale=gout_scales[:], start=True, stop=True)
+        cs = ps.tile([P, I], F32, name="cs")
+        for j in range(I // P):
+            sized = tile("sized%d" % j, [P, Q], F32)
+            nc.scalar.activation(sized[:], c0_turned[:, j, :], ACT.Copy, scale=size_cols[:, j:j + 1])
+            nc.tensor.transpose(cs[:, j * P:(j + 1) * P], sized[:], identity[:])
+
+        wta = tile("wta", [P, I], F32)
+        tau = column("tau")
+        nc.vector.scalar_tensor_tensor(wta[:], ta[:], 1.0, wa[:], op0=ALU.mult, op1=ALU.mult, accum_out=tau[:])
+        ut = tile("ut", [P, I], F32)
+        nc.vector.scalar_tensor_tensor(ut[:], ta[:], tau[:], tanh[:], op0=ALU.subtract, op1=ALU.mult)
+        wcs = tile("wcs", [P, I], F32)
+        nc.vector.tensor_tensor(wcs[:], cs[:], wa[:], ALU.mult)
+        neg_wg = tile("neg_wg", [P, I], F32)
+        neg_g = column("neg_g")
+        nc.vector.scalar_tensor_tensor(neg_wg[:], share_sq[:], -512.0, wcs[:], op0=ALU.mult, op1=ALU.mult,
+                                       accum_out=neg_g[:])
+        z = tile("z", [P, I], F32)
+        h = column("h")
+        nc.vector.scalar_tensor_tensor(z[:], neg_wg[:], -1.0, ut[:], op0=ALU.mult, op1=ALU.mult, accum_out=h[:])
+        neg_g_tau = column("neg_g_tau")
+        g_tau = column("g_tau")
+        wa_factor = column("wa_factor")
+        nc.scalar.activation(neg_g_tau[:], neg_g[:], ACT.Copy, scale=tau[:])
+        nc.scalar.activation(g_tau[:], neg_g_tau[:], ACT.Copy, scale=-1.0)
+        nc.scalar.activation(wa_factor[:], h[:], ACT.Identity, bias=g_tau[:], scale=-1.0)
+        first = tile("first", [P, I], F32)
+        second = tile("second", [P, I], F32)
+        nc.vector.scalar_tensor_tensor(first[:], wta[:], neg_g[:], z[:], op0=ALU.mult, op1=ALU.add)
+        nc.scalar.activation(second[:], wa[:], ACT.Copy, scale=wa_factor[:])
+        nc.vector.tensor_tensor(placed[:].indirect(offsets[:]), first[:], second[:], ALU.add)
+
+        for c in range(T // OUT_CHUNK):
+            cols = slice(c * OUT_CHUNK, (c + 1) * OUT_CHUNK)
+            result = tile("result%d" % c, [P, OUT_CHUNK], F32)
+            nc.vector.tensor_tensor(result[:], placed[:, cols], base_sb[:, cols], ALU.add)
+            queue = nc.sync if c % 2 == 0 else nc.scalar
+            queue.dma_start(out=out[:, cols], in_=result[:])

@@ -24,7 +24,7 @@ TERMS = 36
 STEPS = TERMS + 4
 EXPONENT_BITS = 0x7F800000
 SIGN_AND_EXPONENT_BITS = -0x00800000
-OUT_CHUNK = 512
+OUT_CHUNKS = (256, 512, 512, 512, 256)
 
 
 def tile_attend_hvagreement_s_kernel(tc, query, query2, keys_words, keys_scales, gout, vals_words, vals_scales,
@@ -34,8 +34,10 @@ def tile_attend_hvagreement_s_kernel(tc, query, query2, keys_words, keys_scales,
         sb = ctx.enter_context(tc.tile_pool(name="sb", bufs=1))
         ps = ctx.enter_context(tc.psum_pool(name="ps", bufs=1))
 
-        def tile(name, shape, dtype):
-            return sb.tile(shape, dtype, name=name, align_bytes=64)
+        reused = ctx.enter_context(tc.tile_pool(name="reused", bufs=1))
+
+        def tile(name, shape, dtype, tag=None):
+            return sb.tile(shape, dtype, name=name, tag=tag or name, align_bytes=64)
 
         def column(name):
             return sb.tile([P, 1], F32, name=name)
@@ -43,7 +45,7 @@ def tile_attend_hvagreement_s_kernel(tc, query, query2, keys_words, keys_scales,
         offsets = sb.tile([P, I // 16], U16, name="offsets")
         key_words = tile("key_words", [P, T], U16)
         key_scales = tile("key_scales", [P, T], U8)
-        val_words = tile("val_words", [P, T], U16)
+        val_words = reused.tile([P, T], U16, name="val_words", offset=0)
         val_scales = tile("val_scales", [P, T], U8)
         placed = tile("placed", [P, T], F32)
         base_sb = tile("base_sb", [P, T], F32)
@@ -52,8 +54,11 @@ def tile_attend_hvagreement_s_kernel(tc, query, query2, keys_words, keys_scales,
         nc.vector.memset(key_scales[:].bitcast(I32), 0)
         nc.vector.memset(val_scales[:].bitcast(I32), 0)
 
-        def load_words(dst, src):
-            nc.sync.dma_start(out=dst[:].bitcast(I32), in_=src[0].bitcast(I32))
+        def load_words(dst, src, pieces):
+            width = T // 2 // pieces
+            for piece in range(pieces):
+                cols = slice(piece * width, (piece + 1) * width)
+                nc.sync.dma_start(out=dst[:].bitcast(I32)[:, cols], in_=src[0].bitcast(I32)[:, cols])
 
         def load_scales(dst, src):
             for quad in range(4):
@@ -66,14 +71,14 @@ def tile_attend_hvagreement_s_kernel(tc, query, query2, keys_words, keys_scales,
             return raw
 
         nc.sync.dma_start(offsets[:], offs)
-        load_words(key_words, keys_words)
+        load_words(key_words, keys_words, 1)
         load_scales(key_scales, keys_scales)
         query_raw = load_rows("query", query)
         query2_raw = load_rows("query2", query2)
-        dquery_raw = load_rows("dquery", dquery)
-        gout_raw = load_rows("gout", gout)
-        load_words(val_words, vals_words)
         load_scales(val_scales, vals_scales)
+        gout_raw = load_rows("gout", gout)
+        dquery_raw = load_rows("dquery", dquery)
+        load_words(val_words, vals_words, 1)
         with nc.allow_non_contiguous_dma(reason="one weight a partition"):
             nc.sync.dma_start(out=size_cols[:], in_=size.rearrange("o (j s) -> s (o j)", s=P))
         nc.sync.dma_start(out=base_sb[:], in_=base)
@@ -124,17 +129,16 @@ def tile_attend_hvagreement_s_kernel(tc, query, query2, keys_words, keys_scales,
 
         query_g = interleave("query", query_raw)
         query2_g = interleave("query2", query2_raw)
-        dquery_g = interleave("dquery", dquery_raw)
         gout_g = interleave("gout", gout_raw)
+        dquery_g = interleave("dquery", dquery_raw)
 
         kw = gather("kw", key_words, U16)
         ks = gather("ks", key_scales, U8)
         a = score("a", quantize("query", query_g))
         b = score("b", quantize("query2", query2_g))
-        ta = score("ta", quantize("dquery", dquery_g))
-        gout_codes, gout_scales = quantize("gout", gout_g)
+        vs = gather("vs", val_scales, U8)
 
-        neg_a = tile("neg_a", [P, I], F32)
+        neg_a = tile("neg_a", [P, I], F32, tag="val_scales")
         neg_b = tile("neg_b", [P, I], F32)
         nc.vector.tensor_scalar(neg_a[:], a[:], -1.0, None, op0=ALU.mult, op1=ALU.min, accum_out=neg_max_a)
         nc.vector.tensor_scalar(neg_b[:], b[:], -1.0, None, op0=ALU.mult, op1=ALU.min, accum_out=neg_max_b)
@@ -144,18 +148,30 @@ def tile_attend_hvagreement_s_kernel(tc, query, query2, keys_words, keys_scales,
         sum_b = column("sum_b")
         nc.scalar.activation(pa[:], neg_a[:], ACT.Exp, bias=neg_max_a, scale=-1.0, accum_out=sum_a[:])
         nc.scalar.activation(pb[:], neg_b[:], ACT.Exp, bias=neg_max_b, scale=-1.0, accum_out=sum_b[:])
-        gap = tile("gap", [P, I], F32)
-        nc.vector.tensor_tensor(gap[:], b[:], neg_a[:], ALU.add)
+
         inv_a = column("inv_a")
         nc.vector.reciprocal(inv_a[:], sum_a[:])
+        gout_codes, gout_scales = quantize("gout", gout_g)
+        ta = score("ta", quantize("dquery", dquery_g))
+        vw = gather("vw", val_words, U16)
+        c0_turned = []
+        for j in range(I // P):
+            slots = slice(j * P, (j + 1) * P)
+            bank = ps.tile([P, Q], F32, name="c0_turned%d" % j)
+            nc.tensor.matmul_mx(out=bank[:], lhsT=vw[:, slots].bitcast(FP4X4), lhsT_scale=vs[:, slots],
+                                rhs=gout_codes[:].bitcast(FP8X4), rhs_scale=gout_scales[:], start=True, stop=True)
+            c0_turned.append(bank)
+
+        ratio = tile("ratio", [P, 1], F32)
+        nc.scalar.activation(ratio[:], sum_b[:], ACT.Copy, scale=inv_a[:])
         wa = tile("wa", [P, I], F32)
         nc.scalar.activation(wa[:], pa[:], ACT.Copy, scale=inv_a[:])
 
-        ratio = column("ratio")
-        power = sb.tile([P, 1], I32, name="power")
-        nc.vector.tensor_tensor(ratio[:], sum_b[:], inv_a[:], ALU.mult)
+        power = reused.tile([P, 1], I32, name="power", offset=4 * I)
         nc.vector.tensor_scalar(power[:], ratio[:].bitcast(I32), EXPONENT_BITS, SIGN_AND_EXPONENT_BITS,
                                 op0=ALU.bitwise_and, op1=ALU.bitwise_xor)
+        gap = reused.tile([P, I], F32, name="gap", offset=0)
+        nc.vector.tensor_tensor(gap[:], b[:], neg_a[:], ALU.add)
         nc.vector.tensor_scalar(factors[:, :TERMS + 1], ratio[:].to_broadcast([P, TERMS + 1]), power[:].bitcast(F32), 3.0,
                                 op0=ALU.mult, op1=ALU.add)
         nc.vector.tensor_scalar(addends[:, TERMS:TERMS + 1], power[:], (129.0 - math.log2(3.0)) * 2.0 ** 23,
@@ -167,48 +183,36 @@ def tile_attend_hvagreement_s_kernel(tc, query, query2, keys_words, keys_scales,
         nc.scalar.activation(tanh[:], gap[:], ACT.Tanh, bias=horner[:, STEPS - 1:], scale=0.5)
         nc.scalar.activation(share_sq[:], tanh[:], ACT.Square, bias=half, scale=0.5)
 
-        vw = gather("vw", val_words, U16)
-        vs = gather("vs", val_scales, U8)
-        c0_turned = ps.tile([P, I // P, Q], F32, name="c0_turned")
-        for j in range(I // P):
-            slots = slice(j * P, (j + 1) * P)
-            nc.tensor.matmul_mx(out=c0_turned[:, j, :], lhsT=vw[:, slots].bitcast(FP4X4), lhsT_scale=vs[:, slots],
-                                rhs=gout_codes[:].bitcast(FP8X4), rhs_scale=gout_scales[:], start=True, stop=True)
         cs = ps.tile([P, I], F32, name="cs")
         for j in range(I // P):
             sized = tile("sized%d" % j, [P, Q], F32)
-            nc.scalar.activation(sized[:], c0_turned[:, j, :], ACT.Copy, scale=size_cols[:, j:j + 1])
+            nc.scalar.activation(sized[:], c0_turned[j][:], ACT.Copy, scale=size_cols[:, j:j + 1])
             nc.tensor.transpose(cs[:, j * P:(j + 1) * P], sized[:], identity[:])
 
-        wta = tile("wta", [P, I], F32)
-        tau = column("tau")
-        nc.vector.scalar_tensor_tensor(wta[:], ta[:], 1.0, wa[:], op0=ALU.mult, op1=ALU.mult, accum_out=tau[:])
-        ut = tile("ut", [P, I], F32)
-        nc.vector.scalar_tensor_tensor(ut[:], ta[:], tau[:], tanh[:], op0=ALU.subtract, op1=ALU.mult)
+        neg_wta = tile("neg_wta", [P, I], F32, tag="ratio")
+        ut = tile("ut", [P, I + 1], F32)
+        neg_tau = ut[:, I:]
+        nc.vector.scalar_tensor_tensor(neg_wta[:], ta[:], -1.0, wa[:], op0=ALU.mult, op1=ALU.mult, accum_out=neg_tau)
         wcs = tile("wcs", [P, I], F32)
         nc.vector.tensor_tensor(wcs[:], cs[:], wa[:], ALU.mult)
-        neg_wg = tile("neg_wg", [P, I], F32)
-        neg_g = column("neg_g")
-        nc.vector.scalar_tensor_tensor(neg_wg[:], share_sq[:], -512.0, wcs[:], op0=ALU.mult, op1=ALU.mult,
-                                       accum_out=neg_g[:])
-        z = tile("z", [P, I], F32)
-        h = column("h")
-        nc.vector.scalar_tensor_tensor(z[:], neg_wg[:], -1.0, ut[:], op0=ALU.mult, op1=ALU.mult, accum_out=h[:])
-        neg_g_tau = column("neg_g_tau")
-        g_tau = column("g_tau")
+        wg = tile("wg", [P, I + 1], F32)
+        g = wg[:, I:]
+        nc.vector.scalar_tensor_tensor(wg[:, :I], share_sq[:], 512.0, wcs[:], op0=ALU.mult, op1=ALU.mult, accum_out=g)
+        nc.vector.scalar_tensor_tensor(ut[:, :I], ta[:], neg_tau, tanh[:], op0=ALU.add, op1=ALU.mult)
+        neg_z = tile("neg_z", [P, I + 1], F32)
         wa_factor = column("wa_factor")
-        nc.scalar.activation(neg_g_tau[:], neg_g[:], ACT.Copy, scale=tau[:])
-        nc.scalar.activation(g_tau[:], neg_g_tau[:], ACT.Copy, scale=-1.0)
-        nc.scalar.activation(wa_factor[:], h[:], ACT.Identity, bias=g_tau[:], scale=-1.0)
+        nc.vector.scalar_tensor_tensor(neg_z[:], wg[:], -1.0, ut[:], op0=ALU.mult, op1=ALU.mult, accum_out=wa_factor[:])
         first = tile("first", [P, I], F32)
         second = tile("second", [P, I], F32)
-        nc.vector.scalar_tensor_tensor(first[:], wta[:], neg_g[:], z[:], op0=ALU.mult, op1=ALU.add)
+        nc.vector.scalar_tensor_tensor(first[:], neg_wta[:], g, neg_z[:, :I], op0=ALU.mult, op1=ALU.subtract)
         nc.scalar.activation(second[:], wa[:], ACT.Copy, scale=wa_factor[:])
         nc.vector.tensor_tensor(placed[:].indirect(offsets[:]), first[:], second[:], ALU.add)
 
-        for c in range(T // OUT_CHUNK):
-            cols = slice(c * OUT_CHUNK, (c + 1) * OUT_CHUNK)
-            result = tile("result%d" % c, [P, OUT_CHUNK], F32)
+        start = 0
+        for c, width in enumerate(OUT_CHUNKS):
+            cols = slice(start, start + width)
+            start = start + width
+            result = tile("result%d" % c, [P, width], F32)
             nc.vector.tensor_tensor(result[:], placed[:, cols], base_sb[:, cols], ALU.add)
             queue = nc.sync if c % 2 == 0 else nc.scalar
             queue.dma_start(out=out[:, cols], in_=result[:])

import math
from contextlib import ExitStack

import concourse.mybir as mybir
from concourse.masks import make_identity

D, T, I, Q = 512, 2048, 512, 128
P = 128
PACK = 4
FLOPS = 4 * 2 * D * Q * I

F32 = mybir.dt.float32
BF16 = mybir.dt.bfloat16
I32 = mybir.dt.int32
U32 = mybir.dt.uint32
U16 = mybir.dt.uint16
U8 = mybir.dt.uint8
FP8X4 = mybir.dt.float8_e4m3fn_x4
FP4X4 = mybir.dt.float4_e2m1fn_x4
ALU = mybir.AluOpType
ACT = mybir.ActivationFunctionType

TERMS = 36
STEPS = TERMS + 4
EXPONENT_BITS = 0x7F800000
SIGN_AND_EXPONENT_BITS = -0x00800000
OUT_CHUNKS = (256, 512, 512, 512, 256)


def tile_attend_hvagreement_s_kernel(tc, query, query2, keys_words, keys_scales, gout, vals_words, vals_scales,
                                      size, dquery, base, offs, out):
    nc = tc.nc
    with ExitStack() as ctx:
        sb = ctx.enter_context(tc.tile_pool(name="sb", bufs=1))
        ps = ctx.enter_context(tc.psum_pool(name="ps", bufs=1))

        reused = ctx.enter_context(tc.tile_pool(name="reused", bufs=1))

        def tile(name, shape, dtype, tag=None):
            return sb.tile(shape, dtype, name=name, tag=tag or name, align_bytes=64)

        def column(name):
            return sb.tile([P, 1], F32, name=name)

        offsets = sb.tile([P, I // 16], U16, name="offsets")
        key_words = tile("key_words", [P, T], U16)
        key_scales = tile("key_scales", [P, T], U8)
        val_words = reused.tile([P, T], U16, name="val_words", offset=0)
        val_scales = tile("val_scales", [P, T], U8)
        placed = tile("placed", [P, T], F32)
        base_sb = tile("base_sb", [P, T], F32)
        size_cols = tile("size_cols", [P, I // P], F32)

        nc.vector.memset(key_scales[:].bitcast(I32), 0)
        nc.vector.memset(val_scales[:].bitcast(I32), 0)

        def load_words(dst, src, pieces):
            width = T // 2 // pieces
            for piece in range(pieces):
                cols = slice(piece * width, (piece + 1) * width)
                nc.sync.dma_start(out=dst[:].bitcast(I32)[:, cols], in_=src[0].bitcast(I32)[:, cols])

        def load_scales(dst, src):
            for quad in range(4):
                nc.sync.dma_start(out=dst[32 * quad:32 * quad + 4, :].bitcast(I32),
                                  in_=src[0, 4 * quad:4 * quad + 4, :].bitcast(I32))

        def load_rows(name, src):
            raw = tile(name + "_raw", [P, PACK, Q], F32)
            nc.sync.dma_start(out=raw[:], in_=src.rearrange("(p j) q -> p j q", j=PACK))
            return raw

        nc.sync.dma_start(offsets[:], offs)
        load_words(key_words, keys_words, 1)
        load_scales(key_scales, keys_scales)
        query_raw = load_rows("query", query)
        query2_raw = load_rows("query2", query2)
        load_scales(val_scales, vals_scales)
        gout_raw = load_rows("gout", gout)
        dquery_raw = load_rows("dquery", dquery)
        load_words(val_words, vals_words, 1)
        with nc.allow_non_contiguous_dma(reason="one weight a partition"):
            nc.sync.dma_start(out=size_cols[:], in_=size.rearrange("o (j s) -> s (o j)", s=P))
        nc.sync.dma_start(out=base_sb[:], in_=base)

        orders = tile("orders", [P, TERMS], F32)
        nc.gpsimd.iota(orders[:], pattern=[[-1, TERMS]], base=TERMS, channel_multiplier=0,
                       allow_small_or_imprecise_dtypes=True)
        identity = tile("identity", [P, P], F32)
        make_identity(nc, identity[:])
        thirds = tile("thirds", [P, TERMS], F32)
        nc.scalar.activation(thirds[:], orders[:], ACT.Exp, scale=-math.log(3.0))
        factors = tile("factors", [P, STEPS], F32)
        addends = tile("addends", [P, STEPS], F32)
        inverse_orders = tile("inverse_orders", [P, TERMS], F32)
        nc.vector.memset(placed[:], 0.0)
        nc.vector.memset(factors[:, TERMS + 1:TERMS + 3], -1.0)
        nc.vector.memset(factors[:, TERMS + 3:], 0.5)
        nc.vector.memset(addends[:, TERMS + 3:], 0.0)
        nc.vector.reciprocal(inverse_orders[:], orders[:])
        nc.vector.tensor_tensor(addends[:, :TERMS], thirds[:], inverse_orders[:], ALU.mult)
        half = factors[:, TERMS + 3:]
        neg_max_a = addends[:, TERMS + 1:TERMS + 2]
        neg_max_b = addends[:, TERMS + 2:TERMS + 3]

        def interleave(name, raw):
            grouped = tile(name + "_grouped", [P, Q, PACK], BF16)
            nc.scalar.copy(grouped[:].rearrange("p (c i) j -> p c j i", i=4),
                           raw[:].rearrange("p j (c i) -> p c j i", i=4))
            return grouped

        def quantize(name, grouped):
            codes = tile(name + "_codes", [P, Q], U32)
            scales = tile(name + "_scales", [P, Q], U8)
            nc.vector.quantize_mx(out=codes[:].bitcast(FP8X4), scales=scales[:],
                                  in_=grouped[:].rearrange("p q j -> p (q j)"))
            return codes, scales

        def gather(name, window, dtype):
            picked = tile(name, [P, I], dtype)
            nc.vector.tensor_copy(picked[:], window[:].indirect(offsets[:]))
            return picked

        def score(name, rows):
            bank = ps.tile([P, I], F32, name=name)
            nc.tensor.matmul_mx(out=bank[:], lhsT=rows[0][:].bitcast(FP8X4), lhsT_scale=rows[1][:],
                                rhs=kw[:].bitcast(FP4X4), rhs_scale=ks[:], start=True, stop=True)
            return bank

        query_g = interleave("query", query_raw)
        query2_g = interleave("query2", query2_raw)
        gout_g = interleave("gout", gout_raw)
        dquery_g = interleave("dquery", dquery_raw)

        kw = gather("kw", key_words, U16)
        ks = gather("ks", key_scales, U8)
        a = score("a", quantize("query", query_g))
        b = score("b", quantize("query2", query2_g))
        vs = gather("vs", val_scales, U8)

        neg_a = tile("neg_a", [P, I], F32, tag="val_scales")
        neg_b = tile("neg_b", [P, I], F32)
        nc.vector.tensor_scalar(neg_a[:], a[:], -1.0, None, op0=ALU.mult, op1=ALU.min, accum_out=neg_max_a)
        nc.vector.tensor_scalar(neg_b[:], b[:], -1.0, None, op0=ALU.mult, op1=ALU.min, accum_out=neg_max_b)
        pa = tile("pa", [P, I], F32)
        pb = tile("pb", [P, I], F32)
        sum_a = column("sum_a")
        sum_b = column("sum_b")
        nc.scalar.activation(pa[:], neg_a[:], ACT.Exp, bias=neg_max_a, scale=-1.0, accum_out=sum_a[:])
        nc.scalar.activation(pb[:], neg_b[:], ACT.Exp, bias=neg_max_b, scale=-1.0, accum_out=sum_b[:])

        inv_a = column("inv_a")
        nc.vector.reciprocal(inv_a[:], sum_a[:])
        gout_codes, gout_scales = quantize("gout", gout_g)
        ta = score("ta", quantize("dquery", dquery_g))
        vw = gather("vw", val_words, U16)
        c0_turned = []
        for j in range(I // P):
            slots = slice(j * P, (j + 1) * P)
            bank = ps.tile([P, Q], F32, name="c0_turned%d" % j)
            nc.tensor.matmul_mx(out=bank[:], lhsT=vw[:, slots].bitcast(FP4X4), lhsT_scale=vs[:, slots],
                                rhs=gout_codes[:].bitcast(FP8X4), rhs_scale=gout_scales[:], start=True, stop=True)
            c0_turned.append(bank)

        ratio = tile("ratio", [P, 1], F32)
        nc.scalar.activation(ratio[:], sum_b[:], ACT.Copy, scale=inv_a[:])
        wa = tile("wa", [P, I], F32)
        nc.scalar.activation(wa[:], pa[:], ACT.Copy, scale=inv_a[:])

        power = reused.tile([P, 1], I32, name="power", offset=4 * I)
        nc.vector.tensor_scalar(power[:], ratio[:].bitcast(I32), EXPONENT_BITS, SIGN_AND_EXPONENT_BITS,
                                op0=ALU.bitwise_and, op1=ALU.bitwise_xor)
        gap = reused.tile([P, I], F32, name="gap", offset=0)
        nc.vector.tensor_tensor(gap[:], b[:], neg_a[:], ALU.add)
        nc.vector.tensor_scalar(factors[:, :TERMS + 1], ratio[:].to_broadcast([P, TERMS + 1]), power[:].bitcast(F32), 3.0,
                                op0=ALU.mult, op1=ALU.add)
        nc.vector.tensor_scalar(addends[:, TERMS:TERMS + 1], power[:], (129.0 - math.log2(3.0)) * 2.0 ** 23,
                                math.log(2.0) / 2.0 ** 23, op0=ALU.add, op1=ALU.mult)
        horner = tile("horner", [P, STEPS], F32)
        nc.vector.tensor_tensor_scan(horner[:], factors[:], addends[:], 0.0, op0=ALU.mult, op1=ALU.add)
        tanh = tile("tanh", [P, I], F32)
        share_sq = tile("share_sq", [P, I], F32)
        nc.scalar.activation(tanh[:], gap[:], ACT.Tanh, bias=horner[:, STEPS - 1:], scale=0.5)
        nc.scalar.activation(share_sq[:], tanh[:], ACT.Square, bias=half, scale=0.5)

        cs = ps.tile([P, I], F32, name="cs")
        for j in range(I // P):
            sized = tile("sized%d" % j, [P, Q], F32)
            nc.scalar.activation(sized[:], c0_turned[j][:], ACT.Copy, scale=size_cols[:, j:j + 1])
            nc.tensor.transpose(cs[:, j * P:(j + 1) * P], sized[:], identity[:])

        neg_wta = tile("neg_wta", [P, I], F32, tag="ratio")
        ut = tile("ut", [P, I + 1], F32)
        neg_tau = ut[:, I:]
        nc.vector.scalar_tensor_tensor(neg_wta[:], ta[:], -1.0, wa[:], op0=ALU.mult, op1=ALU.mult, accum_out=neg_tau)
        wcs = tile("wcs", [P, I], F32)
        nc.vector.tensor_tensor(wcs[:], cs[:], wa[:], ALU.mult)
        wg = tile("wg", [P, I + 1], F32)
        g = wg[:, I:]
        nc.vector.scalar_tensor_tensor(wg[:, :I], share_sq[:], 512.0, wcs[:], op0=ALU.mult, op1=ALU.mult, accum_out=g)
        nc.vector.scalar_tensor_tensor(ut[:, :I], ta[:], neg_tau, tanh[:], op0=ALU.add, op1=ALU.mult)
        neg_z = tile("neg_z", [P, I + 1], F32)
        wa_factor = column("wa_factor")
        nc.vector.scalar_tensor_tensor(neg_z[:], wg[:], -1.0, ut[:], op0=ALU.mult, op1=ALU.mult, accum_out=wa_factor[:])
        first = tile("first", [P, I], F32)
        second = tile("second", [P, I], F32)
        nc.vector.scalar_tensor_tensor(first[:], neg_wta[:], g, neg_z[:, :I], op0=ALU.mult, op1=ALU.subtract)
        nc.scalar.activation(second[:], wa[:], ACT.Copy, scale=wa_factor[:])
        nc.vector.tensor_tensor(placed[:].indirect(offsets[:]), first[:], second[:], ALU.add)

        start = 0
        for c, width in enumerate(OUT_CHUNKS):
            cols = slice(start, start + width)
            start = start + width
            result = tile("result%d" % c, [P, width], F32)
            nc.vector.tensor_tensor(result[:], placed[:, cols], base_sb[:, cols], ALU.add)
            queue = nc.sync if c % 2 == 0 else nc.scalar
            queue.dma_start(out=out[:, cols], in_=result[:])
